import numpy as np
import ml_dtypes


def mxq(x, axis, fmt="e4m3"):
    dtype, down = {"e4m3": (ml_dtypes.float8_e4m3fn, 7), "e5m2": (ml_dtypes.float8_e5m2, 14)}[fmt]
    v = np.moveaxis(np.asarray(x, np.float32).astype(ml_dtypes.bfloat16).astype(np.float64), axis, -1)
    blocks = v.reshape(v.shape[:-1] + (-1, 32))
    amax = np.abs(blocks).max(-1, keepdims=True)
    byte = np.maximum(np.where(amax > 0, np.frexp(amax)[1] - 1 + 127, 0) - down, 1)
    scale = np.exp2(byte - 127.0)
    codes = (blocks / scale).astype(np.float32).astype(dtype).astype(np.float64)
    return np.moveaxis((codes * scale).reshape(v.shape), -1, axis)


WIDE = False


def mx_kscale(k):
    if not WIDE:
        return np.ones(k)
    levels = np.array([10, -10, 5, -5, 0])
    if k % 512:
        return np.exp2(np.random.permutation(np.resize(levels, k // 32))).repeat(32)
    a = np.empty((k // 512, 16))
    for p in range(k // 512):
        a[p, :8] = np.random.permutation(np.resize(levels, 8))
        for g in range(8):
            far = levels[np.abs(levels - a[p, g]) >= 10]
            a[p, g + 8] = far[np.random.randint(len(far))]
    return np.exp2(a.ravel()).repeat(32)


def f64(x):
    return np.asarray(x).astype(np.float64)


def striped(idx):
    return np.tile(idx.reshape(-1, 16).T, (8, 1)).astype(np.uint16)


def unstriped(offs):
    return offs[:16].T.reshape(-1).astype(np.int64)


E2M1 = np.array([0.0, 0.5, 1.0, 1.5, 2.0, 3.0, 4.0, 6.0, -0.0, -0.5, -1.0, -1.5, -2.0, -3.0, -4.0, -6.0])


def pack_weight(w, fmt):
    k, n = w.shape
    w = f64(np.asarray(w, np.float32).astype(ml_dtypes.bfloat16)).reshape(k // 32, 32, n)
    amax = np.abs(w).max(1)
    if fmt == "e4m3":
        byte = np.frexp(amax)[1] - 1 + 127 - 7
    else:
        mant, ex = np.frexp(amax / 6.0)
        byte = np.where(mant > 0.5, ex, ex - 1) + 127
    byte = np.clip(np.where(amax > 0, byte, 1), 1, 254)
    scaled = (w * np.exp2(127.0 - byte)[:, None, :]).reshape(k, n).astype(np.float32)
    by_word = np.ascontiguousarray(scaled.reshape(k // 512, 128, 4, n).transpose(0, 1, 3, 2))
    if fmt == "e4m3":
        words = by_word.astype(ml_dtypes.float8_e4m3fn).view(np.uint8)
    else:
        c = by_word.astype(ml_dtypes.float4_e2m1fn).view(np.uint8) & 0xF
        words = (c[..., 0::2] | (c[..., 1::2] << 4)).reshape(k // 512, 128, 2 * n)
    return np.ascontiguousarray(words), np.ascontiguousarray(byte.astype(np.uint8).reshape(k // 512, 16, n))


def unpack_weight(words, scales, fmt):
    g, _, n = scales.shape
    words = np.ascontiguousarray(words).reshape(g, 128, n, -1)
    if fmt == "e4m3":
        vals = words.view(ml_dtypes.float8_e4m3fn).astype(np.float64)
    else:
        nib = np.empty((g, 128, n, 4), np.uint8)
        nib[..., 0::2] = words & 0xF
        nib[..., 1::2] = words >> 4
        vals = E2M1[nib]
    vals = vals * np.repeat(np.exp2(scales.astype(np.float64) - 127.0), 8, axis=1)[..., None]
    return vals.transpose(0, 1, 3, 2).reshape(g * 512, n)


def gelu(v):
    return 0.5 * v * (1.0 + np.tanh(np.sqrt(2.0 / np.pi) * (v + 0.044715 * v**3)))


K, KA, H, T, S, T3, S2, P = 1024, 512, 1024, 2048, 1024, 1024, 512, 512

def setup_inputs():
    n = np.random.standard_normal
    s = mx_kscale(K)[:, None]
    u = mx_kscale(H)[:, None]
    w = n((K, H)) * 1.5 / np.sqrt(K) / s
    tab_words, tab_scales = pack_weight(n((K, T)) * s, "e4m3")
    tab2_words, tab2_scales = pack_weight(n((H, T3)) / np.sqrt(H) / u, "e4m3")
    w4_words, w4_scales = pack_weight(w[:KA], "e2m1")
    return {
        "tab_words": tab_words, "tab_scales": tab_scales,
        "offs": striped(np.random.permutation(T)[:S]),
        "tab2_words": tab2_words, "tab2_scales": tab2_scales,
        "offs2": striped(np.random.permutation(T3)[:S2]),
        "pos1": striped(np.random.permutation(S)[:P]),
        "pos2": striped(np.random.permutation(S)[:P]),
        "w4_words": w4_words, "w4_scales": w4_scales,
        "w1": w[KA:].astype(np.float32),
        "gain": (np.exp(0.3 * n(H)) * u[:, 0]).astype(np.float32),
        "lean": (1.0 + 0.5 * n(H)).astype(np.float32),
        "shift": (0.5 * n(H) * u[:, 0]).astype(np.float32),
        "d1": (1.0 + 0.4 * n(S2)).astype(np.float32),
        "d2": (1.0 + 0.4 * n(S2)).astype(np.float32),
    }

def reference(tab_words, tab_scales, offs, tab2_words, tab2_scales, offs2, pos1, pos2,
              w4_words, w4_scales, w1, gain, lean, shift, d1, d2):
    v = unpack_weight(tab_words, tab_scales, "e4m3")[:, unstriped(offs)]
    v2 = unpack_weight(tab2_words, tab2_scales, "e4m3")[:, unstriped(offs2)]
    w4 = unpack_weight(w4_words, w4_scales, "e2m1")
    wq = mxq(f64(w1), 0, "e4m3")
    h = f64(gain)[:, None] * np.tanh(w4.T @ v[:KA] + wq.T @ v[KA:])
    x1 = mxq(f64(lean)[:, None] * h[:, unstriped(pos1)] + f64(shift)[:, None], 0, "e4m3")
    x2 = mxq(h[:, unstriped(pos2)], 0, "e4m3")
    e1 = v2.T @ x1
    e2 = v2.T @ x2
    return f64(d1)[:, None] * e1 + f64(d2)[:, None] * e2

@@ -1,0 +1,281 @@
+from contextlib import ExitStack
+
+import concourse.mybir as mybir
+
+F32 = mybir.dt.float32
+BF16 = mybir.dt.bfloat16
+I32 = mybir.dt.int32
+U32 = mybir.dt.uint32
+U16 = mybir.dt.uint16
+U8 = mybir.dt.uint8
+FP8X4 = mybir.dt.float8_e4m3fn_x4
+FP4X4 = mybir.dt.float4_e2m1fn_x4
+ACT = mybir.ActivationFunctionType
+ALU = mybir.AluOpType
+
+P = 128
+H, T, S, T3, S2, NP = 1024, 2048, 1024, 1024, 512, 512
+BANK = 512
+HALF = NP // 2
+
+FLOPS = 2 * 1024 * H * S + 2 * 2 * H * S2 * NP
+
+
+def tile_list_omakase_piece_scores_kernel(
+    tc, tab_words, tab_scales, offs, tab2_words, tab2_scales, offs2, pos1, pos2,
+    w4_words, w4_scales, w1, gain, lean, shift, d1, d2, out,
+):
+    nc = tc.nc
+    with ExitStack() as ctx:
+        sb = ctx.enter_context(tc.tile_pool(name="sb", bufs=1))
+        psum = ctx.enter_context(tc.psum_pool(name="psum", bufs=1))
+
+        def new(name, shape, dtype, tag=None):
+            return sb.tile(shape, dtype, name=name, tag=tag or name, align_bytes=64)
+
+        def bank(n):
+            return psum.tile([P, BANK], F32, name="bank%d" % n)
+
+        def load_words(name, words, cols):
+            t = new(name, [P, cols], U32)
+            nc.sync.dma_start(out=t[:].bitcast(I32), in_=words.rearrange("p t i -> p (t i)").bitcast(I32))
+            return t
+
+        def load_scale_rows(queue, plane, scales):
+            passes = scales.shape[0]
+            for q in range(4):
+                queue.dma_start(
+                    out=plane[32 * q : 32 * q + 4 * passes, :].bitcast(I32),
+                    in_=scales[:, 4 * q : 4 * q + 4, :].bitcast(I32),
+                )
+
+        def load_list(name, src):
+            t = sb.tile([P, src.shape[1]], U16, name=name)
+            nc.sync.dma_start(t[:], src)
+            return t
+
+        def load_w1(b):
+            t = new("w1_raw%d" % b, [P, 4, BANK], F32)
+            nc.sync.dma_start(out=t[:], in_=w1[:, BANK * b : BANK * (b + 1)].rearrange("(p j) c -> p j c", j=4))
+            return t
+
+        def load_rows(name, vec):
+            t = new(name, [P, 2, 4], F32)
+            nc.sync.dma_start(out=t[:], in_=vec.rearrange("(b p i) -> p b i", b=2, i=4))
+            return t
+
+        def load_cols(name, vec):
+            t = new(name, [P, 4], F32)
+            with nc.allow_non_contiguous_dma(reason="one value a partition and row tile"):
+                nc.sync.dma_start(out=t[:], in_=vec.rearrange("(m p) -> p m", p=P))
+            return t
+
+        tab_sc = new("tab_sc", [P, T], U8)
+        w4_sc_raw = new("w4_sc_raw", [P, H], U8)
+        tab2_sc = new("tab2_sc", [P, T3], U8)
+        for plane in (tab_sc, w4_sc_raw, tab2_sc):
+            nc.vector.memset(plane[:].bitcast(I32), 0)
+        load_scale_rows(nc.scalar, tab_sc, tab_scales)
+        load_scale_rows(nc.scalar, w4_sc_raw, w4_scales)
+
+        idx = load_list("idx", offs)
+        tab_w0 = load_words("tab_w0", tab_words[0], T)
+        w1_raw = [load_w1(0)]
+        w4_raw = new("w4_raw", [P, 2 * H], U8)
+        nc.sync.dma_start(out=w4_raw[:].bitcast(I32), in_=w4_words[0].bitcast(I32))
+        tab_w1 = load_words("tab_w1", tab_words[1], T)
+        w1_raw.append(load_w1(1))
+        p1 = load_list("p1", pos1)
+        gain_sb = load_rows("gain_sb", gain)
+        lean_sb = load_rows("lean_sb", lean)
+        shift_sb = load_rows("shift_sb", shift)
+        idx2 = load_list("idx2", offs2)
+        load_scale_rows(nc.sync, tab2_sc, tab2_scales)
+        tab2_w = [load_words("tab2_w%d" % a, tab2_words[a], T3) for a in range(2)]
+        p2 = load_list("p2", pos2)
+        d1_sb = load_cols("d1_sb", d1)
+        d2_sb = load_cols("d2_sb", d2)
+
+        v_w = [new("v_w%d" % a, [P, S], U32) for a in range(2)]
+        v_sc = new("v_sc", [P, S], U8)
+        nc.vector.tensor_copy(v_w[0][:], tab_w0[:].indirect(idx[:]))
+        nc.vector.tensor_copy(v_sc[:], tab_sc[:].indirect(idx[:]))
+
+        w4_w = new("w4_w", [P, 2 * H], U8)
+        nc.vector.tensor_copy(
+            out=w4_w[:].bitcast(U16).rearrange("p (b i q) -> p b i q", b=2, i=4),
+            in_=w4_raw[:].bitcast(U16).rearrange("p (b q i) -> p b i q", b=2, i=4),
+        )
+        w4_sc = new("w4_sc", [P, H], U8)
+        nc.vector.tensor_copy(
+            out=w4_sc[:].rearrange("p (b i q) -> p b i q", b=2, i=4),
+            in_=w4_sc_raw[:].rearrange("p (b q i) -> p b i q", b=2, i=4),
+        )
+
+        w1_bf = [new("w1_bf%d" % b, [P, 4 * BANK], BF16) for b in range(2)]
+        w1_w = [new("w1_w%d" % b, [P, BANK], U32) for b in range(2)]
+        w1_sc = [new("w1_sc%d" % b, [P, BANK], U8) for b in range(2)]
+
+        def round_w1(copy, b):
+            copy(
+                out=w1_bf[b][:].rearrange("p (i q j) -> p q j i", i=4, j=4),
+                in_=w1_raw[b][:].rearrange("p j (q i) -> p q j i", i=4),
+            )
+
+        def quantize(words, plane, src):
+            nc.vector.quantize_mx(out=words.bitcast(FP8X4), scales=plane, in_=src)
+
+        round_w1(nc.scalar.copy, 0)
+        quantize(w1_w[0][:], w1_sc[0][:], w1_bf[0][:])
+        for c in range(2):
+            nc.vector.tensor_copy(
+                v_w[1][:, BANK * c : BANK * (c + 1)], tab_w1[:].indirect(idx[:, 32 * c : 32 * (c + 1)])
+            )
+        round_w1(nc.vector.tensor_copy, 1)
+        quantize(w1_w[1][:], w1_sc[1][:], w1_bf[1][:])
+        v2_sc = new("v2_sc", [P, S2], U8)
+        lg_sb = new("lg_sb", [P, 2, 4], F32)
+        nc.vector.tensor_tensor(lg_sb[:], lean_sb[:], gain_sb[:], ALU.mult)
+
+        th = [new("th%d" % k, [P, S], F32) for k in range(8)]
+
+        def first_stage(k):
+            b, i = divmod(k, 4)
+            rows = slice(P * k, P * (k + 1))
+            for c in range(2):
+                cols = slice(BANK * c, BANK * (c + 1))
+                acc = bank((2 * k + c) % 8)
+                nc.tensor.matmul_mx(
+                    out=acc[:], lhsT=w4_w[:, 2 * P * k : 2 * P * (k + 1)].bitcast(FP4X4), lhsT_scale=w4_sc[:, rows],
+                    rhs=v_w[0][:, cols].bitcast(FP8X4), rhs_scale=v_sc[:, cols], start=True, stop=False,
+                )
+                nc.tensor.matmul_mx(
+                    out=acc[:], lhsT=w1_w[b][:, P * i : P * (i + 1)].bitcast(FP8X4),
+                    lhsT_scale=w1_sc[b][:, P * i : P * (i + 1)],
+                    rhs=v_w[1][:, cols].bitcast(FP8X4), rhs_scale=v_sc[4:P, cols], start=False, stop=True,
+                )
+                nc.scalar.activation(out=th[k][:, cols], in_=acc[:], func=ACT.Tanh)
+
+        def pick(dst, k, lst):
+            nc.vector.tensor_copy(dst, th[k][:].indirect(lst))
+            return dst
+
+        def lean_plane(dst, g, k):
+            b, i = divmod(k, 4)
+            nc.scalar.activation(
+                out=dst, in_=g, func=ACT.Identity, scale=lg_sb[:, b, i : i + 1], bias=shift_sb[:, b, i : i + 1]
+            )
+
+        def fat_plane(dst, g, k):
+            b, i = divmod(k, 4)
+            nc.scalar.activation(out=dst, in_=g, func=ACT.Copy, scale=gain_sb[:, b, i : i + 1])
+
+        def fat_plane_v(dst, g, k):
+            b, i = divmod(k, 4)
+            nc.vector.tensor_scalar(dst, g, gain_sb[:, b, i : i + 1], None, ALU.mult)
+
+        def weave(copy, name, planes, n):
+            t = new(name, [P, 4 * n], BF16)
+            copy(
+                out=t[:].rearrange("p (c u i) -> p c i u", u=4, i=4),
+                in_=planes[:].rearrange("p (i c u) -> p c i u", i=4, u=4),
+            )
+            return t
+
+        def quantized(name, src, n):
+            words = new(name + "_w", [P, n], U32)
+            plane = new(name + "_sc", [P, n], U8)
+            quantize(words[:], plane[:], src[:])
+            return words, plane
+
+        v2_w = [new("v2_w%d" % a, [P, S2], U32) for a in range(2)]
+
+        def second(acc, m, b, x, cols, start, stop):
+            rows = slice(P * m, P * (m + 1))
+            nc.tensor.matmul_mx(
+                out=acc, lhsT=v2_w[b][:, rows].bitcast(FP8X4), lhsT_scale=v2_sc[4 * b : P, rows],
+                rhs=x[0][:, cols].bitcast(FP8X4), rhs_scale=x[1][:, cols], start=start, stop=stop,
+            )
+
+        pl1 = [new("pl1_%d" % b, [P, 4 * NP], BF16) for b in range(2)]
+        pl2 = new("pl2_0", [P, 4 * NP], BF16)
+
+        for k in range(8):
+            first_stage(k)
+        g1_all = new("g1_all", [P, 8, NP], F32)
+        g1 = [pick(g1_all[:, k, :], k, p1[:]) for k in range(8)]
+        nc.vector.tensor_copy(v2_sc[:], tab2_sc[:].indirect(idx2[:]))
+        for a in range(2):
+            nc.vector.tensor_copy(v2_w[a][:], tab2_w[a][:].indirect(idx2[:]))
+
+        x1_bf = []
+        for b in range(2):
+            for i in range(4):
+                lean_plane(pl1[b][:, NP * i : NP * (i + 1)], g1[4 * b + i], 4 * b + i)
+            x1_bf.append(weave(nc.scalar.copy, "x1_bf%d" % b, pl1[b], NP))
+
+        g2_a = new("g2_a", [P, 2, NP], F32)
+        g2 = [pick(g2_a[:, k, :], k, p2[:]) for k in range(2)]
+        x1_0 = quantized("x1_0", x1_bf[0], NP)
+        e1 = [bank(m) for m in range(4)]
+        for m in range(4):
+            second(e1[m][:], m, 0, x1_0, slice(0, NP), True, False)
+        g2_b = new("g2_b", [P, 2, NP], F32, tag="x1_bf0")
+        g2 = g2 + [pick(g2_b[:, k, :], 2 + k, p2[:]) for k in range(2)]
+        x1_1 = quantized("x1_1", x1_bf[1], NP)
+        for m in range(4):
+            second(e1[m][:], m, 1, x1_1, slice(0, NP), False, True)
+        for k in range(4):
+            fat_plane(pl2[:, NP * k : NP * (k + 1)], g2[k], k)
+        x2_bf0 = weave(nc.scalar.copy, "x2_bf0", pl2, NP)
+
+        gh = {}
+        gh_a = new("gh_a", [P, 6, HALF], F32, tag="x1_bf1")
+        for n in range(6):
+            c, i = divmod(n, 4)
+            gh[c, i] = pick(gh_a[:, n, :], 4 + i, p2[:, 16 * c : 16 * (c + 1)])
+        x2_0 = quantized("x2_0", x2_bf0, NP)
+        e2 = [bank(4 + n) for n in range(4)]
+        for c in range(2):
+            for m in range(4):
+                second(
+                    e2[2 * c + m // 2][:, HALF * (m % 2) : HALF * (m % 2 + 1)], m, 0, x2_0,
+                    slice(HALF * c, HALF * (c + 1)), m % 2 == 0, False,
+                )
+        gh_b = new("gh_b", [P, 2, HALF], F32, tag="x2_bf0")
+        for i in range(2, 4):
+            gh[1, i] = pick(gh_b[:, i - 2, :], 4 + i, p2[:, 16:32])
+
+        planes = [new("pl2_1_%d" % c, [P, 4 * HALF], BF16) for c in range(2)]
+        for i in range(4):
+            fat_plane(planes[0][:, HALF * i : HALF * (i + 1)], gh[0, i], 4 + i)
+        x2_bf1 = [weave(nc.scalar.copy, "x2_bf1_0", planes[0], HALF)]
+        part = [new("part%d" % m, [P, NP], F32) for m in range(4)]
+        for c in range(2):
+            cols = slice(HALF * c, HALF * (c + 1))
+            for m in range(4):
+                nc.scalar.activation(
+                    out=part[m][:, cols], in_=e1[m][:, cols], func=ACT.Copy, scale=d1_sb[:, m : m + 1]
+                )
+        for i in range(4):
+            fat_plane_v(planes[1][:, HALF * i : HALF * (i + 1)], gh[1, i], 4 + i)
+        x2_q = [quantized("x2_1_0", x2_bf1[0], HALF)]
+        x2_bf1.append(weave(nc.vector.tensor_copy, "x2_bf1_1", planes[1], HALF))
+        x2_q.append(quantized("x2_1_1", x2_bf1[1], HALF))
+        out_rows = out.rearrange("(m p) j -> p m j", p=P)
+        for c in range(2):
+            cols = slice(HALF * c, HALF * (c + 1))
+            for m in range(4):
+                second(
+                    e2[2 * c + m // 2][:, HALF * (m % 2) : HALF * (m % 2 + 1)], m, 1, x2_q[c],
+                    slice(0, HALF), False, m % 2 == 1,
+                )
+            for pair in range(2):
+                res = new("res%d_%d" % (c, pair), [P, 2, HALF], F32)
+                for u in range(2):
+                    m = 2 * pair + u
+                    nc.vector.scalar_tensor_tensor(
+                        out=res[:, u, :], in0=e2[2 * c + pair][:, HALF * u : HALF * (u + 1)],
+                        scalar=d2_sb[:, m : m + 1], in1=part[m][:, cols], op0=ALU.mult, op1=ALU.add,
+                    )
+                nc.sync.dma_start(out=out_rows[:, 2 * pair : 2 * pair + 2, cols], in_=res[:])

@@ -70,47 +70,48 @@ def tile_list_omakase_piece_scores_kernel(
                 nc.sync.dma_start(out=t[:], in_=vec.rearrange("(m p) -> p m", p=P))
             return t
 
-        tab_sc = new("tab_sc", [P, T], U8)
         w4_sc_raw = new("w4_sc_raw", [P, H], U8)
+        tab_sc = new("tab_sc", [P, T], U8)
         tab2_sc = new("tab2_sc", [P, T3], U8)
         for plane in (tab_sc, w4_sc_raw, tab2_sc):
-            nc.vector.memset(plane[:].bitcast(I32), 0)
+            nc.gpsimd.memset(plane[:].bitcast(I32), 0)
         load_scale_rows(nc.scalar, tab_sc, tab_scales)
         load_scale_rows(nc.scalar, w4_sc_raw, w4_scales)
 
         idx = load_list("idx", offs)
-        tab_w0 = load_words("tab_w0", tab_words[0], T)
-        w1_raw = [load_w1(0)]
         w4_raw = new("w4_raw", [P, 2 * H], U8)
         nc.sync.dma_start(out=w4_raw[:].bitcast(I32), in_=w4_words[0].bitcast(I32))
+        tab_w0 = load_words("tab_w0", tab_words[0], T)
+        w1_raw = [load_w1(0)]
         tab_w1 = load_words("tab_w1", tab_words[1], T)
-        w1_raw.append(load_w1(1))
+        idx2 = load_list("idx2", offs2)
+        load_scale_rows(nc.sync, tab2_sc, tab2_scales)
+        tab2_w = [load_words("tab2_w0", tab2_words[0], T3)]
         p1 = load_list("p1", pos1)
+        p2 = load_list("p2", pos2)
+        w1_raw.append(load_w1(1))
         gain_sb = load_rows("gain_sb", gain)
         lean_sb = load_rows("lean_sb", lean)
         shift_sb = load_rows("shift_sb", shift)
-        idx2 = load_list("idx2", offs2)
-        load_scale_rows(nc.sync, tab2_sc, tab2_scales)
-        tab2_w = [load_words("tab2_w%d" % a, tab2_words[a], T3) for a in range(2)]
-        p2 = load_list("p2", pos2)
+        tab2_w.append(load_words("tab2_w1", tab2_words[1], T3))
         d1_sb = load_cols("d1_sb", d1)
         d2_sb = load_cols("d2_sb", d2)
 
         v_w = [new("v_w%d" % a, [P, S], U32) for a in range(2)]
         v_sc = new("v_sc", [P, S], U8)
-        nc.vector.tensor_copy(v_w[0][:], tab_w0[:].indirect(idx[:]))
-        nc.vector.tensor_copy(v_sc[:], tab_sc[:].indirect(idx[:]))
-
         w4_w = new("w4_w", [P, 2 * H], U8)
         nc.vector.tensor_copy(
             out=w4_w[:].bitcast(U16).rearrange("p (b i q) -> p b i q", b=2, i=4),
             in_=w4_raw[:].bitcast(U16).rearrange("p (b q i) -> p b i q", b=2, i=4),
         )
         w4_sc = new("w4_sc", [P, H], U8)
-        nc.vector.tensor_copy(
+        nc.gpsimd.tensor_copy(
             out=w4_sc[:].rearrange("p (b i q) -> p b i q", b=2, i=4),
             in_=w4_sc_raw[:].rearrange("p (b q i) -> p b i q", b=2, i=4),
         )
+
+        nc.vector.tensor_copy(v_sc[:], tab_sc[:].indirect(idx[:]))
+        nc.vector.tensor_copy(v_w[0][:], tab_w0[:].indirect(idx[:]))
 
         w1_bf = [new("w1_bf%d" % b, [P, 4 * BANK], BF16) for b in range(2)]
         w1_w = [new("w1_w%d" % b, [P, BANK], U32) for b in range(2)]
@@ -131,13 +132,14 @@ def tile_list_omakase_piece_scores_kernel(
             nc.vector.tensor_copy(
                 v_w[1][:, BANK * c : BANK * (c + 1)], tab_w1[:].indirect(idx[:, 32 * c : 32 * (c + 1)])
             )
-        round_w1(nc.vector.tensor_copy, 1)
-        quantize(w1_w[1][:], w1_sc[1][:], w1_bf[1][:])
         v2_sc = new("v2_sc", [P, S2], U8)
+        v2_w = [new("v2_w%d" % a, [P, S2], U32) for a in range(2)]
+        nc.vector.tensor_copy(v2_sc[:], tab2_sc[:].indirect(idx2[:]))
+        nc.vector.tensor_copy(v2_w[0][:], tab2_w[0][:].indirect(idx2[:]))
         lg_sb = new("lg_sb", [P, 2, 4], F32)
-        nc.vector.tensor_tensor(lg_sb[:], lean_sb[:], gain_sb[:], ALU.mult)
+        nc.gpsimd.tensor_tensor(lg_sb[:], lean_sb[:], gain_sb[:], ALU.mult)
 
-        th = [new("th%d" % k, [P, S], F32) for k in range(8)]
+        th = {k: new("th%d" % k, [P, S], F32)[:] for k in (0, 1, 4, 5, 6, 7)}
 
         def first_stage(k):
             b, i = divmod(k, 4)
@@ -157,18 +159,16 @@ def tile_list_omakase_piece_scores_kernel(
                 nc.scalar.activation(out=th[k][:, cols], in_=acc[:], func=ACT.Tanh)
 
         def pick(dst, k, lst):
-            nc.vector.tensor_copy(dst, th[k][:].indirect(lst))
+            nc.vector.tensor_copy(dst, th[k].indirect(lst))
             return dst
 
         def lean_plane(dst, g, k):
             b, i = divmod(k, 4)
-            nc.scalar.activation(
-                out=dst, in_=g, func=ACT.Identity, scale=lg_sb[:, b, i : i + 1], bias=shift_sb[:, b, i : i + 1]
-            )
+            nc.gpsimd.tensor_scalar(dst, g, lg_sb[:, b, i : i + 1], shift_sb[:, b, i : i + 1], ALU.mult, ALU.add)
 
         def fat_plane(dst, g, k):
             b, i = divmod(k, 4)
-            nc.scalar.activation(out=dst, in_=g, func=ACT.Copy, scale=gain_sb[:, b, i : i + 1])
+            nc.gpsimd.tensor_scalar(dst, g, gain_sb[:, b, i : i + 1], 0.0, ALU.mult, ALU.add)
 
         def fat_plane_v(dst, g, k):
             b, i = divmod(k, 4)
@@ -188,8 +188,6 @@ def tile_list_omakase_piece_scores_kernel(
             quantize(words[:], plane[:], src[:])
             return words, plane
 
-        v2_w = [new("v2_w%d" % a, [P, S2], U32) for a in range(2)]
-
         def second(acc, m, b, x, cols, start, stop):
             rows = slice(P * m, P * (m + 1))
             nc.tensor.matmul_mx(
@@ -200,40 +198,42 @@ def tile_list_omakase_piece_scores_kernel(
         pl1 = [new("pl1_%d" % b, [P, 4 * NP], BF16) for b in range(2)]
         pl2 = new("pl2_0", [P, 4 * NP], BF16)
 
-        for k in range(8):
-            first_stage(k)
         g1_all = new("g1_all", [P, 8, NP], F32)
-        g1 = [pick(g1_all[:, k, :], k, p1[:]) for k in range(8)]
-        nc.vector.tensor_copy(v2_sc[:], tab2_sc[:].indirect(idx2[:]))
-        for a in range(2):
-            nc.vector.tensor_copy(v2_w[a][:], tab2_w[a][:].indirect(idx2[:]))
+        g2_all = new("g2_all", [P, 4, NP], F32)
 
-        x1_bf = []
-        for b in range(2):
-            for i in range(4):
-                lean_plane(pl1[b][:, NP * i : NP * (i + 1)], g1[4 * b + i], 4 * b + i)
-            x1_bf.append(weave(nc.scalar.copy, "x1_bf%d" % b, pl1[b], NP))
+        def lean_rows(k):
+            lean_plane(pl1[k // 4][:, NP * (k % 4) : NP * (k % 4 + 1)], pick(g1_all[:, k, :], k, p1[:]), k)
 
-        g2_a = new("g2_a", [P, 2, NP], F32)
-        g2 = [pick(g2_a[:, k, :], k, p2[:]) for k in range(2)]
-        x1_0 = quantized("x1_0", x1_bf[0], NP)
+        def fat_rows(k):
+            fat_plane(pl2[:, NP * k : NP * (k + 1)], pick(g2_all[:, k, :], k, p2[:]), k)
+
+        for k in range(2):
+            first_stage(k)
+        round_w1(nc.scalar.copy, 1)
+        th23 = new("th23", [P, 2 * S], F32, tag="w1_raw1")
+        th[2] = th23[:, :S]
+        th[3] = th23[:, S:]
+        for k in range(2):
+            lean_rows(k)
+            fat_rows(k)
+        quantize(w1_w[1][:], w1_sc[1][:], w1_bf[1][:])
+        nc.vector.tensor_copy(v2_w[1][:], tab2_w[1][:].indirect(idx2[:]))
+        for k in range(2, 8):
+            first_stage(k)
+        for k in range(2, 4):
+            lean_rows(k)
+            fat_rows(k)
+        for k in range(4, 8):
+            lean_rows(k)
+
+        x1_bf0 = weave(nc.scalar.copy, "x1_bf0", pl1[0], NP)
+        x2_bf0 = weave(nc.scalar.copy, "x2_bf0", pl2, NP)
+        x1_bf1 = weave(nc.scalar.copy, "x1_bf1", pl1[1], NP)
+
+        x1_0 = quantized("x1_0", x1_bf0, NP)
         e1 = [bank(m) for m in range(4)]
         for m in range(4):
             second(e1[m][:], m, 0, x1_0, slice(0, NP), True, False)
-        g2_b = new("g2_b", [P, 2, NP], F32, tag="x1_bf0")
-        g2 = g2 + [pick(g2_b[:, k, :], 2 + k, p2[:]) for k in range(2)]
-        x1_1 = quantized("x1_1", x1_bf[1], NP)
-        for m in range(4):
-            second(e1[m][:], m, 1, x1_1, slice(0, NP), False, True)
-        for k in range(4):
-            fat_plane(pl2[:, NP * k : NP * (k + 1)], g2[k], k)
-        x2_bf0 = weave(nc.scalar.copy, "x2_bf0", pl2, NP)
-
-        gh = {}
-        gh_a = new("gh_a", [P, 6, HALF], F32, tag="x1_bf1")
-        for n in range(6):
-            c, i = divmod(n, 4)
-            gh[c, i] = pick(gh_a[:, n, :], 4 + i, p2[:, 16 * c : 16 * (c + 1)])
         x2_0 = quantized("x2_0", x2_bf0, NP)
         e2 = [bank(4 + n) for n in range(4)]
         for c in range(2):
@@ -242,9 +242,16 @@ def tile_list_omakase_piece_scores_kernel(
                     e2[2 * c + m // 2][:, HALF * (m % 2) : HALF * (m % 2 + 1)], m, 0, x2_0,
                     slice(HALF * c, HALF * (c + 1)), m % 2 == 0, False,
                 )
-        gh_b = new("gh_b", [P, 2, HALF], F32, tag="x2_bf0")
-        for i in range(2, 4):
-            gh[1, i] = pick(gh_b[:, i - 2, :], 4 + i, p2[:, 16:32])
+        gh = {}
+        gh_a = new("gh_a", [P, 4, HALF], F32, tag="x2_bf0")
+        for i in range(4):
+            gh[0, i] = pick(gh_a[:, i, :], 4 + i, p2[:, 0:16])
+        x1_1 = quantized("x1_1", x1_bf1, NP)
+        for m in range(4):
+            second(e1[m][:], m, 1, x1_1, slice(0, NP), False, True)
+        gh_b = new("gh_b", [P, 4, HALF], F32, tag="x1_bf1")
+        for i in range(4):
+            gh[1, i] = pick(gh_b[:, i, :], 4 + i, p2[:, 16:32])
 
         planes = [new("pl2_1_%d" % c, [P, 4 * HALF], BF16) for c in range(2)]
         for i in range(4):

@@ -54,14 +54,14 @@ def tile_list_omakase_piece_scores_kernel(
             nc.sync.dma_start(t[:], src)
             return t
 
-        def load_w1(b):
-            t = new("w1_raw%d" % b, [P, 4, BANK], F32)
-            nc.sync.dma_start(out=t[:], in_=w1[:, BANK * b : BANK * (b + 1)].rearrange("(p j) c -> p j c", j=4))
-            return t
+        def load_w1(first, width):
+            t = new("w1_raw%d" % first, [P, 4, width], F32)
+            nc.sync.dma_start(out=t[:], in_=w1[:, first : first + width].rearrange("(p j) c -> p j c", j=4))
+            return first, width, t
 
-        def load_rows(name, vec):
+        def load_rows(queue, name, vec):
             t = new(name, [P, 2, 4], F32)
-            nc.sync.dma_start(out=t[:], in_=vec.rearrange("(b p i) -> p b i", b=2, i=4))
+            queue.dma_start(out=t[:], in_=vec.rearrange("(b p i) -> p b i", b=2, i=4))
             return t
 
         def load_cols(name, vec):
@@ -73,27 +73,30 @@ def tile_list_omakase_piece_scores_kernel(
         w4_sc_raw = new("w4_sc_raw", [P, H], U8)
         tab_sc = new("tab_sc", [P, T], U8)
         tab2_sc = new("tab2_sc", [P, T3], U8)
-        for plane in (tab_sc, w4_sc_raw, tab2_sc):
-            nc.gpsimd.memset(plane[:].bitcast(I32), 0)
-        load_scale_rows(nc.scalar, tab_sc, tab_scales)
-        load_scale_rows(nc.scalar, w4_sc_raw, w4_scales)
-
+        nc.vector.memset(tab_sc[:].bitcast(I32), 0)
+        nc.vector.memset(w4_sc_raw[:].bitcast(I32), 0)
+        nc.gpsimd.memset(tab2_sc[:].bitcast(I32), 0)
         idx = load_list("idx", offs)
         w4_raw = new("w4_raw", [P, 2 * H], U8)
         nc.sync.dma_start(out=w4_raw[:].bitcast(I32), in_=w4_words[0].bitcast(I32))
+        gain_sb = load_rows(nc.sync, "gain_sb", gain)
         tab_w0 = load_words("tab_w0", tab_words[0], T)
-        w1_raw = [load_w1(0)]
+        load_scale_rows(nc.sync, tab_sc, tab_scales)
         tab_w1 = load_words("tab_w1", tab_words[1], T)
+        load_scale_rows(nc.sync, w4_sc_raw, w4_scales)
+        w1_raw = [load_w1(HALF * n, HALF) for n in range(2)]
         idx2 = load_list("idx2", offs2)
         load_scale_rows(nc.sync, tab2_sc, tab2_scales)
-        tab2_w = [load_words("tab2_w0", tab2_words[0], T3)]
         p1 = load_list("p1", pos1)
         p2 = load_list("p2", pos2)
-        w1_raw.append(load_w1(1))
-        gain_sb = load_rows("gain_sb", gain)
-        lean_sb = load_rows("lean_sb", lean)
-        shift_sb = load_rows("shift_sb", shift)
-        tab2_w.append(load_words("tab2_w1", tab2_words[1], T3))
+        lean_sb = load_rows(nc.sync, "lean_sb", lean)
+        shift_sb = load_rows(nc.sync, "shift_sb", shift)
+        w1_raw.append(load_w1(BANK, BANK))
+        tab2_w = [load_words("tab2_w%d" % a, tab2_words[a], T3) for a in range(2)]
+
+        gain_wide = [new("gain_wide%d" % b, [P, 4, n], F32) for b, n in enumerate((NP, HALF))]
+        for b, n in enumerate((NP, HALF)):
+            nc.scalar.copy(out=gain_wide[b][:], in_=gain_sb[:, b, :].unsqueeze(2).to_broadcast([P, 4, n]))
         d1_sb = load_cols("d1_sb", d1)
         d2_sb = load_cols("d2_sb", d2)
 
@@ -110,36 +113,34 @@ def tile_list_omakase_piece_scores_kernel(
             in_=w4_sc_raw[:].rearrange("p (b q i) -> p b i q", b=2, i=4),
         )
 
-        nc.vector.tensor_copy(v_sc[:], tab_sc[:].indirect(idx[:]))
         nc.vector.tensor_copy(v_w[0][:], tab_w0[:].indirect(idx[:]))
+        nc.vector.tensor_copy(v_sc[:], tab_sc[:].indirect(idx[:]))
 
         w1_bf = [new("w1_bf%d" % b, [P, 4 * BANK], BF16) for b in range(2)]
         w1_w = [new("w1_w%d" % b, [P, BANK], U32) for b in range(2)]
         w1_sc = [new("w1_sc%d" % b, [P, BANK], U8) for b in range(2)]
 
-        def round_w1(copy, b):
-            copy(
-                out=w1_bf[b][:].rearrange("p (i q j) -> p q j i", i=4, j=4),
-                in_=w1_raw[b][:].rearrange("p j (q i) -> p q j i", i=4),
+        def round_w1(first, width, raw):
+            b, c = divmod(first, BANK)
+            nc.scalar.copy(
+                out=w1_bf[b][:].rearrange("p (i q j) -> p q j i", i=4, j=4)[:, c // 4 : (c + width) // 4],
+                in_=raw[:].rearrange("p j (q i) -> p q j i", i=4),
             )
 
         def quantize(words, plane, src):
             nc.vector.quantize_mx(out=words.bitcast(FP8X4), scales=plane, in_=src)
 
-        round_w1(nc.scalar.copy, 0)
+        nc.vector.tensor_copy(v_w[1][:], tab_w1[:].indirect(idx[:]))
+        for piece in w1_raw[:2]:
+            round_w1(*piece)
         quantize(w1_w[0][:], w1_sc[0][:], w1_bf[0][:])
-        for c in range(2):
-            nc.vector.tensor_copy(
-                v_w[1][:, BANK * c : BANK * (c + 1)], tab_w1[:].indirect(idx[:, 32 * c : 32 * (c + 1)])
-            )
         v2_sc = new("v2_sc", [P, S2], U8)
         v2_w = [new("v2_w%d" % a, [P, S2], U32) for a in range(2)]
         nc.vector.tensor_copy(v2_sc[:], tab2_sc[:].indirect(idx2[:]))
-        nc.vector.tensor_copy(v2_w[0][:], tab2_w[0][:].indirect(idx2[:]))
         lg_sb = new("lg_sb", [P, 2, 4], F32)
         nc.gpsimd.tensor_tensor(lg_sb[:], lean_sb[:], gain_sb[:], ALU.mult)
 
-        th = {k: new("th%d" % k, [P, S], F32)[:] for k in (0, 1, 4, 5, 6, 7)}
+        th = [new("th%d" % k, [P, S], F32)[:] for k in range(8)]
 
         def first_stage(k):
             b, i = divmod(k, 4)
@@ -164,18 +165,16 @@ def tile_list_omakase_piece_scores_kernel(
 
         def lean_plane(dst, g, k):
             b, i = divmod(k, 4)
-            nc.gpsimd.tensor_scalar(dst, g, lg_sb[:, b, i : i + 1], shift_sb[:, b, i : i + 1], ALU.mult, ALU.add)
+            nc.scalar.activation(
+                out=dst, in_=g, func=ACT.Identity, scale=lg_sb[:, b, i : i + 1], bias=shift_sb[:, b, i : i + 1]
+            )
 
-        def fat_plane(dst, g, k):
+        def pick_gained(dst, k, lst):
             b, i = divmod(k, 4)
-            nc.gpsimd.tensor_scalar(dst, g, gain_sb[:, b, i : i + 1], 0.0, ALU.mult, ALU.add)
+            nc.vector.tensor_tensor(dst, th[k].indirect(lst), gain_wide[b][:, i, :], ALU.mult)
 
-        def fat_plane_v(dst, g, k):
-            b, i = divmod(k, 4)
-            nc.vector.tensor_scalar(dst, g, gain_sb[:, b, i : i + 1], None, ALU.mult)
-
-        def weave(copy, name, planes, n):
-            t = new(name, [P, 4 * n], BF16)
+        def weave(copy, name, planes, n, tag=None):
+            t = new(name, [P, 4 * n], BF16, tag=tag)
             copy(
                 out=t[:].rearrange("p (c u i) -> p c i u", u=4, i=4),
                 in_=planes[:].rearrange("p (i c u) -> p c i u", i=4, u=4),
@@ -196,44 +195,44 @@ def tile_list_omakase_piece_scores_kernel(
             )
 
         pl1 = [new("pl1_%d" % b, [P, 4 * NP], BF16) for b in range(2)]
-        pl2 = new("pl2_0", [P, 4 * NP], BF16)
 
         g1_all = new("g1_all", [P, 8, NP], F32)
-        g2_all = new("g2_all", [P, 4, NP], F32)
-
-        def lean_rows(k):
-            lean_plane(pl1[k // 4][:, NP * (k % 4) : NP * (k % 4 + 1)], pick(g1_all[:, k, :], k, p1[:]), k)
-
-        def fat_rows(k):
-            fat_plane(pl2[:, NP * k : NP * (k + 1)], pick(g2_all[:, k, :], k, p2[:]), k)
-
-        for k in range(2):
+        for k in range(4):
             first_stage(k)
-        round_w1(nc.scalar.copy, 1)
-        th23 = new("th23", [P, 2 * S], F32, tag="w1_raw1")
-        th[2] = th23[:, :S]
-        th[3] = th23[:, S:]
-        for k in range(2):
-            lean_rows(k)
-            fat_rows(k)
+        round_w1(*w1_raw[2])
+        for k in range(4):
+            pick(g1_all[:, k, :], k, p1[:])
+        nc.vector.tensor_copy(v2_w[0][:], tab2_w[0][:].indirect(idx2[:]))
         quantize(w1_w[1][:], w1_sc[1][:], w1_bf[1][:])
-        nc.vector.tensor_copy(v2_w[1][:], tab2_w[1][:].indirect(idx2[:]))
-        for k in range(2, 8):
-            first_stage(k)
-        for k in range(2, 4):
-            lean_rows(k)
-            fat_rows(k)
         for k in range(4, 8):
-            lean_rows(k)
+            first_stage(k)
+        g2_0 = new("g2_0", [P, 4 * NP], F32, tag="w1_bf1")
+        for k in range(4):
+            pick_gained(g2_0[:, NP * k : NP * (k + 1)], k, p2[:])
+        nc.vector.tensor_copy(v2_w[1][:], tab2_w[1][:].indirect(idx2[:]))
+        for k in range(4, 8):
+            pick(g1_all[:, k, :], k, p1[:])
 
-        x1_bf0 = weave(nc.scalar.copy, "x1_bf0", pl1[0], NP)
-        x2_bf0 = weave(nc.scalar.copy, "x2_bf0", pl2, NP)
-        x1_bf1 = weave(nc.scalar.copy, "x1_bf1", pl1[1], NP)
+        def lean_block(b):
+            for i in range(4):
+                lean_plane(pl1[b][:, NP * i : NP * (i + 1)], g1_all[:, 4 * b + i, :], 4 * b + i)
+            return weave(nc.scalar.copy, "x1_bf%d" % b, pl1[b], NP)
+
+        x1_bf0 = lean_block(0)
+        x2_bf0 = weave(nc.scalar.copy, "x2_bf0", g2_0, NP)
+        x1_bf1 = lean_block(1)
+
+        def fat_half(c, tag):
+            g = new("g2_1_%d" % c, [P, 4 * HALF], F32, tag=tag)
+            for i in range(4):
+                pick_gained(g[:, HALF * i : HALF * (i + 1)], 4 + i, p2[:, 16 * c : 16 * (c + 1)])
+            return g
 
         x1_0 = quantized("x1_0", x1_bf0, NP)
         e1 = [bank(m) for m in range(4)]
         for m in range(4):
             second(e1[m][:], m, 0, x1_0, slice(0, NP), True, False)
+        gh = [fat_half(0, "x1_bf0")]
         x2_0 = quantized("x2_0", x2_bf0, NP)
         e2 = [bank(4 + n) for n in range(4)]
         for c in range(2):
@@ -242,21 +241,12 @@ def tile_list_omakase_piece_scores_kernel(
                     e2[2 * c + m // 2][:, HALF * (m % 2) : HALF * (m % 2 + 1)], m, 0, x2_0,
                     slice(HALF * c, HALF * (c + 1)), m % 2 == 0, False,
                 )
-        gh = {}
-        gh_a = new("gh_a", [P, 4, HALF], F32, tag="x2_bf0")
-        for i in range(4):
-            gh[0, i] = pick(gh_a[:, i, :], 4 + i, p2[:, 0:16])
+        gh.append(fat_half(1, "x2_bf0"))
         x1_1 = quantized("x1_1", x1_bf1, NP)
         for m in range(4):
             second(e1[m][:], m, 1, x1_1, slice(0, NP), False, True)
-        gh_b = new("gh_b", [P, 4, HALF], F32, tag="x1_bf1")
-        for i in range(4):
-            gh[1, i] = pick(gh_b[:, i, :], 4 + i, p2[:, 16:32])
 
-        planes = [new("pl2_1_%d" % c, [P, 4 * HALF], BF16) for c in range(2)]
-        for i in range(4):
-            fat_plane(planes[0][:, HALF * i : HALF * (i + 1)], gh[0, i], 4 + i)
-        x2_bf1 = [weave(nc.scalar.copy, "x2_bf1_0", planes[0], HALF)]
+        x2_bf1 = [weave(nc.scalar.copy, "x2_bf1_0", gh[0], HALF)]
         part = [new("part%d" % m, [P, NP], F32) for m in range(4)]
         for c in range(2):
             cols = slice(HALF * c, HALF * (c + 1))
@@ -264,11 +254,8 @@ def tile_list_omakase_piece_scores_kernel(
                 nc.scalar.activation(
                     out=part[m][:, cols], in_=e1[m][:, cols], func=ACT.Copy, scale=d1_sb[:, m : m + 1]
                 )
-        for i in range(4):
-            fat_plane_v(planes[1][:, HALF * i : HALF * (i + 1)], gh[1, i], 4 + i)
-        x2_q = [quantized("x2_1_0", x2_bf1[0], HALF)]
-        x2_bf1.append(weave(nc.vector.tensor_copy, "x2_bf1_1", planes[1], HALF))
-        x2_q.append(quantized("x2_1_1", x2_bf1[1], HALF))
+        x2_bf1.append(weave(nc.vector.tensor_copy, "x2_bf1_1", gh[1], HALF, tag="x1_bf1"))
+        x2_q = [quantized("x2_1_%d" % c, x2_bf1[c], HALF) for c in range(2)]
         out_rows = out.rearrange("(m p) j -> p m j", p=P)
         for c in range(2):
             cols = slice(HALF * c, HALF * (c + 1))

@@ -57,7 +57,7 @@ def tile_list_omakase_piece_scores_kernel(
         def load_w1(first, width):
             t = new("w1_raw%d" % first, [P, 4, width], F32)
             nc.sync.dma_start(out=t[:], in_=w1[:, first : first + width].rearrange("(p j) c -> p j c", j=4))
-            return first, width, t
+            return t
 
         def load_rows(queue, name, vec):
             t = new(name, [P, 2, 4], F32)
@@ -73,26 +73,28 @@ def tile_list_omakase_piece_scores_kernel(
         w4_sc_raw = new("w4_sc_raw", [P, H], U8)
         tab_sc = new("tab_sc", [P, T], U8)
         tab2_sc = new("tab2_sc", [P, T3], U8)
-        nc.vector.memset(tab_sc[:].bitcast(I32), 0)
+        nc.gpsimd.memset(tab_sc[:].bitcast(I32), 0)
+        nc.vector.memset(tab2_sc[:].bitcast(I32), 0)
         nc.vector.memset(w4_sc_raw[:].bitcast(I32), 0)
-        nc.gpsimd.memset(tab2_sc[:].bitcast(I32), 0)
+
         idx = load_list("idx", offs)
         w4_raw = new("w4_raw", [P, 2 * H], U8)
         nc.sync.dma_start(out=w4_raw[:].bitcast(I32), in_=w4_words[0].bitcast(I32))
         gain_sb = load_rows(nc.sync, "gain_sb", gain)
-        tab_w0 = load_words("tab_w0", tab_words[0], T)
         load_scale_rows(nc.sync, tab_sc, tab_scales)
-        tab_w1 = load_words("tab_w1", tab_words[1], T)
-        load_scale_rows(nc.sync, w4_sc_raw, w4_scales)
-        w1_raw = [load_w1(HALF * n, HALF) for n in range(2)]
+        tab_w0 = load_words("tab_w0", tab_words[0], T)
         idx2 = load_list("idx2", offs2)
         load_scale_rows(nc.sync, tab2_sc, tab2_scales)
+        w1_raw = [load_w1(0, BANK)]
+        load_scale_rows(nc.sync, w4_sc_raw, w4_scales)
+        tab_w1 = load_words("tab_w1", tab_words[1], T)
+        tab2_w = [load_words("tab2_w0", tab2_words[0], T3)]
         p1 = load_list("p1", pos1)
-        p2 = load_list("p2", pos2)
+        w1_raw.append(load_w1(BANK, BANK))
+        tab2_w.append(load_words("tab2_w1", tab2_words[1], T3))
         lean_sb = load_rows(nc.sync, "lean_sb", lean)
         shift_sb = load_rows(nc.sync, "shift_sb", shift)
-        w1_raw.append(load_w1(BANK, BANK))
-        tab2_w = [load_words("tab2_w%d" % a, tab2_words[a], T3) for a in range(2)]
+        p2 = load_list("p2", pos2)
 
         gain_wide = [new("gain_wide%d" % b, [P, 4, n], F32) for b, n in enumerate((NP, HALF))]
         for b, n in enumerate((NP, HALF)):
@@ -113,30 +115,33 @@ def tile_list_omakase_piece_scores_kernel(
             in_=w4_sc_raw[:].rearrange("p (b q i) -> p b i q", b=2, i=4),
         )
 
-        nc.vector.tensor_copy(v_w[0][:], tab_w0[:].indirect(idx[:]))
         nc.vector.tensor_copy(v_sc[:], tab_sc[:].indirect(idx[:]))
+        nc.vector.tensor_copy(v_w[0][:], tab_w0[:].indirect(idx[:]))
+        v2_sc = new("v2_sc", [P, S2], U8)
+        nc.vector.tensor_copy(v2_sc[:], tab2_sc[:].indirect(idx2[:]))
 
         w1_bf = [new("w1_bf%d" % b, [P, 4 * BANK], BF16) for b in range(2)]
         w1_w = [new("w1_w%d" % b, [P, BANK], U32) for b in range(2)]
         w1_sc = [new("w1_sc%d" % b, [P, BANK], U8) for b in range(2)]
 
-        def round_w1(first, width, raw):
-            b, c = divmod(first, BANK)
-            nc.scalar.copy(
-                out=w1_bf[b][:].rearrange("p (i q j) -> p q j i", i=4, j=4)[:, c // 4 : (c + width) // 4],
-                in_=raw[:].rearrange("p j (q i) -> p q j i", i=4),
+        def round_w1(copy, b, rows):
+            copy(
+                out=w1_bf[b][:].rearrange("p (i q j) -> p q j i", i=4, j=4)[:, rows],
+                in_=w1_raw[b][:].rearrange("p j (q i) -> p q j i", i=4)[:, rows],
             )
 
         def quantize(words, plane, src):
             nc.vector.quantize_mx(out=words.bitcast(FP8X4), scales=plane, in_=src)
 
-        nc.vector.tensor_copy(v_w[1][:], tab_w1[:].indirect(idx[:]))
-        for piece in w1_raw[:2]:
-            round_w1(*piece)
+        round_w1(nc.scalar.copy, 0, slice(0, 64))
+        round_w1(nc.vector.tensor_copy, 0, slice(64, P))
         quantize(w1_w[0][:], w1_sc[0][:], w1_bf[0][:])
-        v2_sc = new("v2_sc", [P, S2], U8)
+        for c in range(2):
+            nc.vector.tensor_copy(
+                v_w[1][:, BANK * c : BANK * (c + 1)], tab_w1[:].indirect(idx[:, 32 * c : 32 * (c + 1)])
+            )
         v2_w = [new("v2_w%d" % a, [P, S2], U32) for a in range(2)]
-        nc.vector.tensor_copy(v2_sc[:], tab2_sc[:].indirect(idx2[:]))
+        nc.vector.tensor_copy(v2_w[0][:], tab2_w[0][:].indirect(idx2[:]))
         lg_sb = new("lg_sb", [P, 2, 4], F32)
         nc.gpsimd.tensor_tensor(lg_sb[:], lean_sb[:], gain_sb[:], ALU.mult)
 
@@ -165,9 +170,11 @@ def tile_list_omakase_piece_scores_kernel(
 
         def lean_plane(dst, g, k):
             b, i = divmod(k, 4)
-            nc.scalar.activation(
-                out=dst, in_=g, func=ACT.Identity, scale=lg_sb[:, b, i : i + 1], bias=shift_sb[:, b, i : i + 1]
-            )
+            scale, bias = lg_sb[:, b, i : i + 1], shift_sb[:, b, i : i + 1]
+            if k == 7:
+                nc.scalar.activation(out=dst, in_=g, func=ACT.Identity, scale=scale, bias=bias)
+            else:
+                nc.gpsimd.tensor_scalar(dst, g, scale, bias, ALU.mult, ALU.add)
 
         def pick_gained(dst, k, lst):
             b, i = divmod(k, 4)
@@ -199,17 +206,16 @@ def tile_list_omakase_piece_scores_kernel(
         g1_all = new("g1_all", [P, 8, NP], F32)
         for k in range(4):
             first_stage(k)
-        round_w1(*w1_raw[2])
+        round_w1(nc.scalar.copy, 1, slice(0, P))
         for k in range(4):
             pick(g1_all[:, k, :], k, p1[:])
-        nc.vector.tensor_copy(v2_w[0][:], tab2_w[0][:].indirect(idx2[:]))
+        nc.vector.tensor_copy(v2_w[1][:], tab2_w[1][:].indirect(idx2[:]))
         quantize(w1_w[1][:], w1_sc[1][:], w1_bf[1][:])
         for k in range(4, 8):
             first_stage(k)
         g2_0 = new("g2_0", [P, 4 * NP], F32, tag="w1_bf1")
         for k in range(4):
             pick_gained(g2_0[:, NP * k : NP * (k + 1)], k, p2[:])
-        nc.vector.tensor_copy(v2_w[1][:], tab2_w[1][:].indirect(idx2[:]))
         for k in range(4, 8):
             pick(g1_all[:, k, :], k, p1[:])
 
@@ -232,7 +238,6 @@ def tile_list_omakase_piece_scores_kernel(
         e1 = [bank(m) for m in range(4)]
         for m in range(4):
             second(e1[m][:], m, 0, x1_0, slice(0, NP), True, False)
-        gh = [fat_half(0, "x1_bf0")]
         x2_0 = quantized("x2_0", x2_bf0, NP)
         e2 = [bank(4 + n) for n in range(4)]
         for c in range(2):
@@ -241,10 +246,11 @@ def tile_list_omakase_piece_scores_kernel(
                     e2[2 * c + m // 2][:, HALF * (m % 2) : HALF * (m % 2 + 1)], m, 0, x2_0,
                     slice(HALF * c, HALF * (c + 1)), m % 2 == 0, False,
                 )
-        gh.append(fat_half(1, "x2_bf0"))
+        gh = [fat_half(0, "x2_bf0")]
         x1_1 = quantized("x1_1", x1_bf1, NP)
         for m in range(4):
             second(e1[m][:], m, 1, x1_1, slice(0, NP), False, True)
+        gh.append(fat_half(1, "x1_bf1"))
 
         x2_bf1 = [weave(nc.scalar.copy, "x2_bf1_0", gh[0], HALF)]
         part = [new("part%d" % m, [P, NP], F32) for m in range(4)]
@@ -254,9 +260,9 @@ def tile_list_omakase_piece_scores_kernel(
                 nc.scalar.activation(
                     out=part[m][:, cols], in_=e1[m][:, cols], func=ACT.Copy, scale=d1_sb[:, m : m + 1]
                 )
-        x2_bf1.append(weave(nc.vector.tensor_copy, "x2_bf1_1", gh[1], HALF, tag="x1_bf1"))
-        x2_q = [quantized("x2_1_%d" % c, x2_bf1[c], HALF) for c in range(2)]
-        out_rows = out.rearrange("(m p) j -> p m j", p=P)
+        x2_q = [quantized("x2_1_0", x2_bf1[0], HALF)]
+        x2_bf1.append(weave(nc.vector.tensor_copy, "x2_bf1_1", gh[1], HALF))
+        x2_q.append(quantized("x2_1_1", x2_bf1[1], HALF))
         for c in range(2):
             cols = slice(HALF * c, HALF * (c + 1))
             for m in range(4):
@@ -264,12 +270,10 @@ def tile_list_omakase_piece_scores_kernel(
                     e2[2 * c + m // 2][:, HALF * (m % 2) : HALF * (m % 2 + 1)], m, 1, x2_q[c],
                     slice(0, HALF), False, m % 2 == 1,
                 )
-            for pair in range(2):
-                res = new("res%d_%d" % (c, pair), [P, 2, HALF], F32)
-                for u in range(2):
-                    m = 2 * pair + u
-                    nc.vector.scalar_tensor_tensor(
-                        out=res[:, u, :], in0=e2[2 * c + pair][:, HALF * u : HALF * (u + 1)],
-                        scalar=d2_sb[:, m : m + 1], in1=part[m][:, cols], op0=ALU.mult, op1=ALU.add,
-                    )
-                nc.sync.dma_start(out=out_rows[:, 2 * pair : 2 * pair + 2, cols], in_=res[:])
+            for m in range(4):
+                res = new("res%d_%d" % (c, m), [P, HALF], F32)
+                nc.vector.scalar_tensor_tensor(
+                    out=res[:], in0=e2[2 * c + m // 2][:, HALF * (m % 2) : HALF * (m % 2 + 1)],
+                    scalar=d2_sb[:, m : m + 1], in1=part[m][:, cols], op0=ALU.mult, op1=ALU.add,
+                )
+                nc.sync.dma_start(out=out[P * m : P * (m + 1), cols], in_=res[:])

from contextlib import ExitStack

import concourse.mybir as mybir

F32 = mybir.dt.float32
BF16 = mybir.dt.bfloat16
I32 = mybir.dt.int32
U32 = mybir.dt.uint32
U16 = mybir.dt.uint16
U8 = mybir.dt.uint8
FP8X4 = mybir.dt.float8_e4m3fn_x4
FP4X4 = mybir.dt.float4_e2m1fn_x4
ACT = mybir.ActivationFunctionType
ALU = mybir.AluOpType

P = 128
H, T, S, T3, S2, NP = 1024, 2048, 1024, 1024, 512, 512
BANK = 512
HALF = NP // 2

FLOPS = 2 * 1024 * H * S + 2 * 2 * H * S2 * NP


def tile_list_omakase_piece_scores_kernel(
    tc, tab_words, tab_scales, offs, tab2_words, tab2_scales, offs2, pos1, pos2,
    w4_words, w4_scales, w1, gain, lean, shift, d1, d2, out,
):
    nc = tc.nc
    with ExitStack() as ctx:
        sb = ctx.enter_context(tc.tile_pool(name="sb", bufs=1))
        psum = ctx.enter_context(tc.psum_pool(name="psum", bufs=1))

        def new(name, shape, dtype, tag=None):
            return sb.tile(shape, dtype, name=name, tag=tag or name, align_bytes=64)

        def bank(n):
            return psum.tile([P, BANK], F32, name="bank%d" % n)

        def load_words(name, words, cols):
            t = new(name, [P, cols], U32)
            nc.sync.dma_start(out=t[:].bitcast(I32), in_=words.rearrange("p t i -> p (t i)").bitcast(I32))
            return t

        def load_scale_rows(queue, plane, scales):
            passes = scales.shape[0]
            for q in range(4):
                queue.dma_start(
                    out=plane[32 * q : 32 * q + 4 * passes, :].bitcast(I32),
                    in_=scales[:, 4 * q : 4 * q + 4, :].bitcast(I32),
                )

        def load_list(name, src):
            t = sb.tile([P, src.shape[1]], U16, name=name)
            nc.sync.dma_start(t[:], src)
            return t

        def load_w1(first, width):
            t = new("w1_raw%d" % first, [P, 4, width], F32)
            nc.sync.dma_start(out=t[:], in_=w1[:, first : first + width].rearrange("(p j) c -> p j c", j=4))
            return t

        def load_rows(queue, name, vec):
            t = new(name, [P, 2, 4], F32)
            queue.dma_start(out=t[:], in_=vec.rearrange("(b p i) -> p b i", b=2, i=4))
            return t

        def load_cols(name, vec):
            t = new(name, [P, 4], F32)
            with nc.allow_non_contiguous_dma(reason="one value a partition and row tile"):
                nc.sync.dma_start(out=t[:], in_=vec.rearrange("(m p) -> p m", p=P))
            return t

        w4_sc_raw = new("w4_sc_raw", [P, H], U8)
        tab_sc = new("tab_sc", [P, T], U8)
        tab2_sc = new("tab2_sc", [P, T3], U8)
        nc.gpsimd.memset(tab_sc[:].bitcast(I32), 0)
        nc.vector.memset(tab2_sc[:].bitcast(I32), 0)
        nc.vector.memset(w4_sc_raw[:].bitcast(I32), 0)

        idx = load_list("idx", offs)
        w4_raw = new("w4_raw", [P, 2 * H], U8)
        nc.sync.dma_start(out=w4_raw[:].bitcast(I32), in_=w4_words[0].bitcast(I32))
        gain_sb = load_rows(nc.sync, "gain_sb", gain)
        load_scale_rows(nc.sync, tab_sc, tab_scales)
        tab_w0 = load_words("tab_w0", tab_words[0], T)
        idx2 = load_list("idx2", offs2)
        load_scale_rows(nc.sync, tab2_sc, tab2_scales)
        w1_raw = [load_w1(0, BANK)]
        load_scale_rows(nc.sync, w4_sc_raw, w4_scales)
        tab_w1 = load_words("tab_w1", tab_words[1], T)
        tab2_w = [load_words("tab2_w0", tab2_words[0], T3)]
        p1 = load_list("p1", pos1)
        w1_raw.append(load_w1(BANK, BANK))
        tab2_w.append(load_words("tab2_w1", tab2_words[1], T3))
        lean_sb = load_rows(nc.sync, "lean_sb", lean)
        shift_sb = load_rows(nc.sync, "shift_sb", shift)
        p2 = load_list("p2", pos2)

        gain_wide = [new("gain_wide%d" % b, [P, 4, n], F32) for b, n in enumerate((NP, HALF))]
        for b, n in enumerate((NP, HALF)):
            nc.scalar.copy(out=gain_wide[b][:], in_=gain_sb[:, b, :].unsqueeze(2).to_broadcast([P, 4, n]))
        d1_sb = load_cols("d1_sb", d1)
        d2_sb = load_cols("d2_sb", d2)

        v_w = [new("v_w%d" % a, [P, S], U32) for a in range(2)]
        v_sc = new("v_sc", [P, S], U8)
        w4_w = new("w4_w", [P, 2 * H], U8)
        nc.vector.tensor_copy(
            out=w4_w[:].bitcast(U16).rearrange("p (b i q) -> p b i q", b=2, i=4),
            in_=w4_raw[:].bitcast(U16).rearrange("p (b q i) -> p b i q", b=2, i=4),
        )
        w4_sc = new("w4_sc", [P, H], U8)
        nc.gpsimd.tensor_copy(
            out=w4_sc[:].rearrange("p (b i q) -> p b i q", b=2, i=4),
            in_=w4_sc_raw[:].rearrange("p (b q i) -> p b i q", b=2, i=4),
        )

        nc.vector.tensor_copy(v_sc[:], tab_sc[:].indirect(idx[:]))
        nc.vector.tensor_copy(v_w[0][:], tab_w0[:].indirect(idx[:]))
        v2_sc = new("v2_sc", [P, S2], U8)
        nc.vector.tensor_copy(v2_sc[:], tab2_sc[:].indirect(idx2[:]))

        w1_bf = [new("w1_bf%d" % b, [P, 4 * BANK], BF16) for b in range(2)]
        w1_w = [new("w1_w%d" % b, [P, BANK], U32) for b in range(2)]
        w1_sc = [new("w1_sc%d" % b, [P, BANK], U8) for b in range(2)]

        def round_w1(copy, b, rows):
            copy(
                out=w1_bf[b][:].rearrange("p (i q j) -> p q j i", i=4, j=4)[:, rows],
                in_=w1_raw[b][:].rearrange("p j (q i) -> p q j i", i=4)[:, rows],
            )

        def quantize(words, plane, src):
            nc.vector.quantize_mx(out=words.bitcast(FP8X4), scales=plane, in_=src)

        round_w1(nc.scalar.copy, 0, slice(0, 64))
        round_w1(nc.vector.tensor_copy, 0, slice(64, P))
        quantize(w1_w[0][:], w1_sc[0][:], w1_bf[0][:])
        for c in range(2):
            nc.vector.tensor_copy(
                v_w[1][:, BANK * c : BANK * (c + 1)], tab_w1[:].indirect(idx[:, 32 * c : 32 * (c + 1)])
            )
        v2_w = [new("v2_w%d" % a, [P, S2], U32) for a in range(2)]
        nc.vector.tensor_copy(v2_w[0][:], tab2_w[0][:].indirect(idx2[:]))
        lg_sb = new("lg_sb", [P, 2, 4], F32)
        nc.gpsimd.tensor_tensor(lg_sb[:], lean_sb[:], gain_sb[:], ALU.mult)

        th = [new("th%d" % k, [P, S], F32)[:] for k in range(8)]

        def first_stage(k):
            b, i = divmod(k, 4)
            rows = slice(P * k, P * (k + 1))
            for c in range(2):
                cols = slice(BANK * c, BANK * (c + 1))
                acc = bank((2 * k + c) % 8)
                nc.tensor.matmul_mx(
                    out=acc[:], lhsT=w4_w[:, 2 * P * k : 2 * P * (k + 1)].bitcast(FP4X4), lhsT_scale=w4_sc[:, rows],
                    rhs=v_w[0][:, cols].bitcast(FP8X4), rhs_scale=v_sc[:, cols], start=True, stop=False,
                )
                nc.tensor.matmul_mx(
                    out=acc[:], lhsT=w1_w[b][:, P * i : P * (i + 1)].bitcast(FP8X4),
                    lhsT_scale=w1_sc[b][:, P * i : P * (i + 1)],
                    rhs=v_w[1][:, cols].bitcast(FP8X4), rhs_scale=v_sc[4:P, cols], start=False, stop=True,
                )
                nc.scalar.activation(out=th[k][:, cols], in_=acc[:], func=ACT.Tanh)

        def pick(dst, k, lst):
            nc.vector.tensor_copy(dst, th[k].indirect(lst))
            return dst

        def lean_plane(dst, g, k):
            b, i = divmod(k, 4)
            scale, bias = lg_sb[:, b, i : i + 1], shift_sb[:, b, i : i + 1]
            if k == 7:
                nc.scalar.activation(out=dst, in_=g, func=ACT.Identity, scale=scale, bias=bias)
            else:
                nc.gpsimd.tensor_scalar(dst, g, scale, bias, ALU.mult, ALU.add)

        def pick_gained(dst, k, lst):
            b, i = divmod(k, 4)
            nc.vector.tensor_tensor(dst, th[k].indirect(lst), gain_wide[b][:, i, :], ALU.mult)

        def weave(copy, name, planes, n, tag=None):
            t = new(name, [P, 4 * n], BF16, tag=tag)
            copy(
                out=t[:].rearrange("p (c u i) -> p c i u", u=4, i=4),
                in_=planes[:].rearrange("p (i c u) -> p c i u", i=4, u=4),
            )
            return t

        def quantized(name, src, n):
            words = new(name + "_w", [P, n], U32)
            plane = new(name + "_sc", [P, n], U8)
            quantize(words[:], plane[:], src[:])
            return words, plane

        def second(acc, m, b, x, cols, start, stop):
            rows = slice(P * m, P * (m + 1))
            nc.tensor.matmul_mx(
                out=acc, lhsT=v2_w[b][:, rows].bitcast(FP8X4), lhsT_scale=v2_sc[4 * b : P, rows],
                rhs=x[0][:, cols].bitcast(FP8X4), rhs_scale=x[1][:, cols], start=start, stop=stop,
            )

        pl1 = [new("pl1_%d" % b, [P, 4 * NP], BF16) for b in range(2)]

        g1_all = new("g1_all", [P, 8, NP], F32)
        for k in range(4):
            first_stage(k)
        round_w1(nc.scalar.copy, 1, slice(0, P))
        for k in range(4):
            pick(g1_all[:, k, :], k, p1[:])
        nc.vector.tensor_copy(v2_w[1][:], tab2_w[1][:].indirect(idx2[:]))
        quantize(w1_w[1][:], w1_sc[1][:], w1_bf[1][:])
        for k in range(4, 8):
            first_stage(k)
        g2_0 = new("g2_0", [P, 4 * NP], F32, tag="w1_bf1")
        for k in range(4):
            pick_gained(g2_0[:, NP * k : NP * (k + 1)], k, p2[:])
        for k in range(4, 8):
            pick(g1_all[:, k, :], k, p1[:])

        def lean_block(b):
            for i in range(4):
                lean_plane(pl1[b][:, NP * i : NP * (i + 1)], g1_all[:, 4 * b + i, :], 4 * b + i)
            return weave(nc.scalar.copy, "x1_bf%d" % b, pl1[b], NP)

        x1_bf0 = lean_block(0)
        x2_bf0 = weave(nc.scalar.copy, "x2_bf0", g2_0, NP)
        x1_bf1 = lean_block(1)

        def fat_half(c, tag):
            g = new("g2_1_%d" % c, [P, 4 * HALF], F32, tag=tag)
            for i in range(4):
                pick_gained(g[:, HALF * i : HALF * (i + 1)], 4 + i, p2[:, 16 * c : 16 * (c + 1)])
            return g

        x1_0 = quantized("x1_0", x1_bf0, NP)
        e1 = [bank(m) for m in range(4)]
        for m in range(4):
            second(e1[m][:], m, 0, x1_0, slice(0, NP), True, False)
        x2_0 = quantized("x2_0", x2_bf0, NP)
        e2 = [bank(4 + n) for n in range(4)]
        for c in range(2):
            for m in range(4):
                second(
                    e2[2 * c + m // 2][:, HALF * (m % 2) : HALF * (m % 2 + 1)], m, 0, x2_0,
                    slice(HALF * c, HALF * (c + 1)), m % 2 == 0, False,
                )
        gh = [fat_half(0, "x2_bf0")]
        x1_1 = quantized("x1_1", x1_bf1, NP)
        for m in range(4):
            second(e1[m][:], m, 1, x1_1, slice(0, NP), False, True)
        gh.append(fat_half(1, "x1_bf1"))

        x2_bf1 = [weave(nc.scalar.copy, "x2_bf1_0", gh[0], HALF)]
        part = [new("part%d" % m, [P, NP], F32) for m in range(4)]
        for c in range(2):
            cols = slice(HALF * c, HALF * (c + 1))
            for m in range(4):
                nc.scalar.activation(
                    out=part[m][:, cols], in_=e1[m][:, cols], func=ACT.Copy, scale=d1_sb[:, m : m + 1]
                )
        x2_q = [quantized("x2_1_0", x2_bf1[0], HALF)]
        x2_bf1.append(weave(nc.vector.tensor_copy, "x2_bf1_1", gh[1], HALF))
        x2_q.append(quantized("x2_1_1", x2_bf1[1], HALF))
        for c in range(2):
            cols = slice(HALF * c, HALF * (c + 1))
            for m in range(4):
                second(
                    e2[2 * c + m // 2][:, HALF * (m % 2) : HALF * (m % 2 + 1)], m, 1, x2_q[c],
                    slice(0, HALF), False, m % 2 == 1,
                )
            for m in range(4):
                res = new("res%d_%d" % (c, m), [P, HALF], F32)
                nc.vector.scalar_tensor_tensor(
                    out=res[:], in0=e2[2 * c + m // 2][:, HALF * (m % 2) : HALF * (m % 2 + 1)],
                    scalar=d2_sb[:, m : m + 1], in1=part[m][:, cols], op0=ALU.mult, op1=ALU.add,
                )
                nc.sync.dma_start(out=out[P * m : P * (m + 1), cols], in_=res[:])
